import numpy as np
import ml_dtypes


def mxq(x, axis, fmt="e4m3"):
    dtype, down = {"e4m3": (ml_dtypes.float8_e4m3fn, 7), "e5m2": (ml_dtypes.float8_e5m2, 14)}[fmt]
    v = np.moveaxis(np.asarray(x, np.float32).astype(ml_dtypes.bfloat16).astype(np.float64), axis, -1)
    blocks = v.reshape(v.shape[:-1] + (-1, 32))
    amax = np.abs(blocks).max(-1, keepdims=True)
    byte = np.maximum(np.where(amax > 0, np.frexp(amax)[1] - 1 + 127, 0) - down, 1)
    scale = np.exp2(byte - 127.0)
    codes = (blocks / scale).astype(np.float32).astype(dtype).astype(np.float64)
    return np.moveaxis((codes * scale).reshape(v.shape), -1, axis)


WIDE = False


def mx_kscale(k):
    if not WIDE:
        return np.ones(k)
    levels = np.array([10, -10, 5, -5, 0])
    if k % 512:
        return np.exp2(np.random.permutation(np.resize(levels, k // 32))).repeat(32)
    a = np.empty((k // 512, 16))
    for p in range(k // 512):
        a[p, :8] = np.random.permutation(np.resize(levels, 8))
        for g in range(8):
            far = levels[np.abs(levels - a[p, g]) >= 10]
            a[p, g + 8] = far[np.random.randint(len(far))]
    return np.exp2(a.ravel()).repeat(32)


def f64(x):
    return np.asarray(x).astype(np.float64)


def striped(idx):
    return np.tile(idx.reshape(-1, 16).T, (8, 1)).astype(np.uint16)


def unstriped(offs):
    return offs[:16].T.reshape(-1).astype(np.int64)


E2M1 = np.array([0.0, 0.5, 1.0, 1.5, 2.0, 3.0, 4.0, 6.0, -0.0, -0.5, -1.0, -1.5, -2.0, -3.0, -4.0, -6.0])


def pack_weight(w, fmt):
    k, n = w.shape
    w = f64(np.asarray(w, np.float32).astype(ml_dtypes.bfloat16)).reshape(k // 32, 32, n)
    amax = np.abs(w).max(1)
    if fmt == "e4m3":
        byte = np.frexp(amax)[1] - 1 + 127 - 7
    else:
        mant, ex = np.frexp(amax / 6.0)
        byte = np.where(mant > 0.5, ex, ex - 1) + 127
    byte = np.clip(np.where(amax > 0, byte, 1), 1, 254)
    scaled = (w * np.exp2(127.0 - byte)[:, None, :]).reshape(k, n).astype(np.float32)
    by_word = np.ascontiguousarray(scaled.reshape(k // 512, 128, 4, n).transpose(0, 1, 3, 2))
    if fmt == "e4m3":
        words = by_word.astype(ml_dtypes.float8_e4m3fn).view(np.uint8)
    else:
        c = by_word.astype(ml_dtypes.float4_e2m1fn).view(np.uint8) & 0xF
        words = (c[..., 0::2] | (c[..., 1::2] << 4)).reshape(k // 512, 128, 2 * n)
    return np.ascontiguousarray(words), np.ascontiguousarray(byte.astype(np.uint8).reshape(k // 512, 16, n))


def unpack_weight(words, scales, fmt):
    g, _, n = scales.shape
    words = np.ascontiguousarray(words).reshape(g, 128, n, -1)
    if fmt == "e4m3":
        vals = words.view(ml_dtypes.float8_e4m3fn).astype(np.float64)
    else:
        nib = np.empty((g, 128, n, 4), np.uint8)
        nib[..., 0::2] = words & 0xF
        nib[..., 1::2] = words >> 4
        vals = E2M1[nib]
    vals = vals * np.repeat(np.exp2(scales.astype(np.float64) - 127.0), 8, axis=1)[..., None]
    return vals.transpose(0, 1, 3, 2).reshape(g * 512, n)


def gelu(v):
    return 0.5 * v * (1.0 + np.tanh(np.sqrt(2.0 / np.pi) * (v + 0.044715 * v**3)))


K, K2, H, N, T, S = 1024, 512, 1024, 384, 4096, 1024


def setup_inputs():
    n = np.random.standard_normal
    s = mx_kscale(K)[:, None]
    s2 = mx_kscale(K2)[:, None]
    u = mx_kscale(H)[:, None]
    d = {}
    d["tab_words"], d["tab_scales"] = pack_weight(n((K, T)) * s, "e4m3")
    d["offs"] = striped(np.random.permutation(T)[:S])
    d["xs_words"], d["xs_scales"] = pack_weight(n((K2, S)) * s2, "e4m3")
    d["w1"] = (n((K, H)) / K**0.5 / s * u.T).astype(np.float32)
    d["w2"] = (n((K2, H)) / K2**0.5 / s2 * u.T).astype(np.float32)
    d["w3_words"], d["w3_scales"] = pack_weight(n((K2, H)) / K2**0.5 / s2 * u.T, "e2m1")
    d["w4_words"], d["w4_scales"] = pack_weight(1.4 * n((H, N)) / H**0.5 / u, "e2m1")
    d["bias"] = (0.7 * n(N)).astype(np.float32)
    return d


def reference(tab_words, tab_scales, offs, xs_words, xs_scales, w1, w2, w3_words, w3_scales,
              w4_words, w4_scales, bias):
    v = unpack_weight(tab_words, tab_scales, "e4m3")[:, unstriped(offs)]
    xs = unpack_weight(xs_words, xs_scales, "e4m3")
    w3 = unpack_weight(w3_words, w3_scales, "e2m1")
    w4 = unpack_weight(w4_words, w4_scales, "e2m1")
    name = mxq(f64(w1), 0, "e4m3").T @ v
    read1 = mxq(f64(w2), 0, "e4m3").T @ xs
    read2 = w3.T @ xs
    reading = np.maximum(read1, read2)
    h = np.abs(name - reading)
    hq = mxq(h, 0, "e4m3")
    y = (w4.T @ hq) + f64(bias)[:, None]
    return 1.0 / (1.0 + np.exp(-y))

@@ -1,0 +1,342 @@
+from contextlib import ExitStack
+
+import concourse.mybir as mybir
+
+K, K2, H, N, T, S = 1024, 512, 1024, 384, 4096, 1024
+FLOPS = 2 * S * (K * H + 2 * K2 * H + H * N)
+
+F32 = mybir.dt.float32
+BF16 = mybir.dt.bfloat16
+I32 = mybir.dt.int32
+U32 = mybir.dt.uint32
+U16 = mybir.dt.uint16
+U8 = mybir.dt.uint8
+FP8X4 = mybir.dt.float8_e4m3fn_x4
+FP4X4 = mybir.dt.float4_e2m1fn_x4
+ALU = mybir.AluOpType
+ACT = mybir.ActivationFunctionType
+
+P = 128
+PACK = 4
+KP = P * PACK
+BANK = 512
+GROUPS = H // KP
+BINS = N // P
+ABS_WIDTH = 256
+FOLDED = tuple((1, half, t) for half in range(2) for t in range(PACK))[:-1]
+CASTS = {
+    ("w2", 0, 0): ("vector", "scalar"),
+    ("w2", 0, 1): ("scalar", "scalar"),
+    ("w1", 0, 0): ("scalar", "scalar"),
+    ("w1", 1, 0): ("scalar", "vector"),
+    ("w1", 0, 1): ("scalar", "scalar"),
+    ("w1", 1, 1): ("scalar", "scalar"),
+}
+RAW_BYTES = PACK * KP * 4
+LATE_BYTES = 5 * RAW_BYTES + 2 * T * 4 + T + 2 * N * GROUPS + N * GROUPS + 64
+
+
+def tile_list_street_reading_mismatch_kernel(
+    tc, tab_words, tab_scales, offs, xs_words, xs_scales, w1, w2, w3_words, w3_scales, w4_words, w4_scales, bias, out
+):
+    nc = tc.nc
+    with ExitStack() as ctx:
+        keep = ctx.enter_context(tc.tile_pool(name="keep", bufs=1))
+        late = ctx.enter_context(tc.tile_pool(name="late", bufs=1))
+        ring = ctx.enter_context(tc.tile_pool(name="ring", bufs=2))
+        psum = ctx.enter_context(tc.psum_pool(name="psum", bufs=1))
+        banks_used = []
+        late_used = []
+
+        def bank(shape):
+            tag = "bank%d" % (len(banks_used) % 8)
+            banks_used.append(tag)
+            return psum.tile(shape, F32, name=tag, tag=tag)
+
+        def kept(name, shape, dtype):
+            return keep.tile(shape, dtype, name=name, align_bytes=64)
+
+        def late_tile(name, shape, dtype, nbytes):
+            tile = late.tile(shape, dtype, name=name, align_bytes=64, offset=sum(late_used))
+            late_used.append(nbytes)
+            return tile
+
+        offsets = keep.tile([P, S // 16], U16, name="offsets")
+
+        warm_in = keep.tile([P, 8], F32, name="warm_in", tag="xs_s", align_bytes=64)
+        warm_out = keep.tile([P, 8], F32, name="warm_out", tag="xs_c", align_bytes=64)
+        nc.vector.memset(warm_in[:], 0.0)
+        nc.scalar.activation(out=warm_out[:], in_=warm_in[:], func=ACT.Sigmoid)
+
+        xs_s = keep.tile([P, S], U8, name="xs_s", tag="xs_s", align_bytes=64)
+        w3_s_in = kept("w3_s_in", [P, H], U8)
+        nc.vector.memset(w3_s_in[:].bitcast(I32), 0)
+        nc.vector.memset(xs_s[:].bitcast(I32), 0)
+
+        raw = {}
+        tab_c = {}
+
+        def load_weight(key, tile):
+            raw[key] = tile
+            w = w1 if key[0] == "w1" else w2
+            rows = w[key[1] * KP : (key[1] + 1) * KP, key[2] * KP : (key[2] + 1) * KP]
+            nc.sync.dma_start(out=tile[:].rearrange("p (j c) -> p j c", j=PACK), in_=rows.rearrange("(p j) c -> p j c", j=PACK))
+
+        def load_late_weight(key):
+            load_weight(key, late_tile("raw_%s_%d_%d" % key, [P, PACK * KP], F32, RAW_BYTES))
+
+        def load_table(a):
+            tab_c[a] = late_tile("tab_c%d" % a, [P, T], U32, 4 * T)
+            nc.sync.dma_start(out=tab_c[a][:].bitcast(I32), in_=tab_words[a].rearrange("p n t -> p (n t)").bitcast(I32))
+
+        w3_in = late.tile([P, LATE_BYTES], U8, name="w3_in", align_bytes=64, offset=0)
+        nc.sync.dma_start(out=w3_in[:, : 2 * H].bitcast(I32), in_=w3_words[0].bitcast(I32))
+        load_weight(("w2", 0, 0), kept("first_raw", [P, PACK * KP], F32))
+        nc.sync.dma_start(offsets[:], offs)
+        for q in range(4):
+            nc.sync.dma_start(out=w3_s_in[32 * q : 32 * q + 4, :].bitcast(I32), in_=w3_scales[0, 4 * q : 4 * q + 4, :].bitcast(I32))
+        xs_c = keep.tile([P, S], U32, name="xs_c", tag="xs_c", align_bytes=64)
+        nc.sync.dma_start(out=xs_c[:].bitcast(I32), in_=xs_words[0].rearrange("p n t -> p (n t)").bitcast(I32))
+        for q in range(4):
+            nc.sync.dma_start(out=xs_s[32 * q : 32 * q + 4, :].bitcast(I32), in_=xs_scales[0, 4 * q : 4 * q + 4, :].bitcast(I32))
+
+        codes = {}
+        scales = {}
+        grouped = {}
+
+        def cast_weight(key):
+            sign = -1.0 if key[0] == "w2" else 1.0
+            for half, engine in enumerate(CASTS[key]):
+                tag = "picked_c0" if (key, half) == (("w2", 0, 1), 1) else "grouped"
+                pool = keep if tag == "picked_c0" else ring
+                tile = pool.tile([P, 2 * KP], BF16, name="grouped", tag=tag, align_bytes=64, bufs=1 if tag == "picked_c0" else 6)
+                grouped[key, half] = tile
+                order = "p m t j" if engine == "gpsimd" else "p m j t"
+                src = raw[key][:].rearrange("p (j m h t) -> h " + order, j=PACK, h=2, t=2)[half]
+                dst = tile[:].rearrange("p (t m j) -> " + order, j=PACK, t=2)
+                if engine == "scalar":
+                    nc.scalar.activation(out=dst, in_=src, func=ACT.Copy, scale=sign)
+                elif engine == "vector":
+                    nc.vector.tensor_scalar(out=dst, in0=src, scalar1=sign, scalar2=None, op0=ALU.mult)
+                else:
+                    nc.gpsimd.tensor_scalar(out=dst, in0=src, scalar1=sign, scalar2=0.0, op0=ALU.mult, op1=ALU.add)
+
+        def quantize_weight(key):
+            for half in range(2):
+                codes[key, half] = kept("c_%s_%d_%d" % key + "_%d" % half, [P, 2 * P], U32)
+                scales[key, half] = kept("s_%s_%d_%d" % key + "_%d" % half, [P, 2 * P], U8)
+                nc.vector.quantize_mx(out=codes[key, half][:].bitcast(FP8X4), scales=scales[key, half][:], in_=grouped[key, half][:])
+
+        w3_c = kept("w3_c", [P, 2 * H], U8)
+        w3_s = kept("w3_s", [P, H], U8)
+        nc.vector.tensor_copy(
+            out=w3_c[:].bitcast(U16).rearrange("p (b t m) -> p b t m", b=GROUPS, t=PACK),
+            in_=w3_in[:, : 2 * H].bitcast(U16).rearrange("p (b m t) -> p b t m", b=GROUPS, t=PACK),
+        )
+        cast_weight(("w2", 0, 0))
+        nc.vector.tensor_copy(
+            out=w3_s[:].rearrange("p (b t m) -> p b t m", b=GROUPS, t=PACK),
+            in_=w3_s_in[:].rearrange("p (b m t) -> p b t m", b=GROUPS, t=PACK),
+        )
+        quantize_weight(("w2", 0, 0))
+
+        def pass_w2(acc, b, t, cols, start, stop):
+            key = (("w2", 0, b), t // 2)
+            nc.tensor.matmul_mx(
+                out=acc, lhsT=codes[key][:, t % 2 * P : (t % 2 + 1) * P].bitcast(FP8X4), lhsT_scale=scales[key][:, t % 2 * P : (t % 2 + 1) * P],
+                rhs=xs_c[:, cols].bitcast(FP8X4), rhs_scale=xs_s[:, cols], start=start, stop=stop,
+            )
+
+        def pass_w3(acc, b, t, cols, start, stop):
+            m0 = b * KP + t * P
+            nc.tensor.matmul_mx(
+                out=acc, lhsT=w3_c[:, 2 * m0 : 2 * (m0 + P)].bitcast(FP4X4), lhsT_scale=w3_s[:, m0 : m0 + P],
+                rhs=xs_c[:, cols].bitcast(FP8X4), rhs_scale=xs_s[:, cols], start=start, stop=stop,
+            )
+
+        picked_c = {}
+        picked_s = kept("picked_s", [P, S], U8)
+
+        def pass_w1(acc, a, b, t, cols, start, stop):
+            key = (("w1", a, b), t // 2)
+            nc.tensor.matmul_mx(
+                out=acc, lhsT=codes[key][:, t % 2 * P : (t % 2 + 1) * P].bitcast(FP8X4), lhsT_scale=scales[key][:, t % 2 * P : (t % 2 + 1) * P],
+                rhs=picked_c[a][:, cols].bitcast(FP8X4), rhs_scale=picked_s[4 * a : P, cols], start=start, stop=stop,
+            )
+
+        reading = {}
+
+        def readings(b, half):
+            cols = slice(half * BANK, (half + 1) * BANK)
+            reading[b, half] = kept("reading%d%d" % (b, half), [P, PACK, BANK], F32)
+            for t in range(PACK):
+                if (b, half, t) in FOLDED:
+                    acc = bank([P, BANK])
+                    pass_w3(acc[:], b, t, cols, True, False)
+                    pass_w2(acc[:], b, t, cols, False, True)
+                    nc.scalar.activation(out=reading[b, half][:, t, :], in_=acc[:], func=ACT.Relu)
+                else:
+                    acc2 = bank([P, BANK])
+                    pass_w3(acc2[:], b, t, cols, True, True)
+                    read2 = ring.tile([P, BANK], F32, name="read2", bufs=4)
+                    nc.scalar.copy(out=read2[:], in_=acc2[:])
+                    acc1 = bank([P, BANK])
+                    pass_w2(acc1[:], b, t, cols, True, True)
+                    nc.vector.scalar_tensor_tensor(
+                        out=reading[b, half][:, t, :], in0=acc1[:], scalar=-1.0, in1=read2[:], op0=ALU.mult, op1=ALU.max
+                    )
+
+        h_c = [kept("h_c%d" % b, [P, S], U32) for b in range(GROUPS)]
+        h_s = [kept("h_s%d" % b, [P, S], U8) for b in range(GROUPS)]
+        diff = {}
+        h16 = {}
+
+        def difference(b, c0, width):
+            cols = slice(c0, c0 + width)
+            half = c0 // BANK
+            inner = slice(c0 % BANK, c0 % BANK + width)
+            per_bank = BANK // width
+            diff[b, c0] = ring.tile([P, PACK, width], F32, name="diff", bufs=2)
+            for t0 in range(0, PACK, per_bank):
+                acc = bank([P, per_bank, width])
+                for u in range(per_bank):
+                    t = t0 + u
+                    pass_w1(acc[:, u, :], 0, b, t, cols, True, False)
+                    if (b, half, t) in FOLDED:
+                        pass_w2(acc[:, u, :], b, t, cols, False, False)
+                    pass_w1(acc[:, u, :], 1, b, t, cols, False, True)
+                nc.vector.tensor_tensor(
+                    out=diff[b, c0][:, t0 : t0 + per_bank, :], in0=acc[:],
+                    in1=reading[b, half][:, t0 : t0 + per_bank, inner], op=ALU.subtract,
+                )
+            for n0 in range(0, width, ABS_WIDTH):
+                part = min(width, ABS_WIDTH)
+                h16[b, c0 + n0] = ring.tile([P, PACK * part], BF16, name="h16", align_bytes=64, bufs=4)
+                nc.scalar.activation(
+                    out=h16[b, c0 + n0][:].rearrange("p (c i t) -> p c t i", i=4, t=PACK),
+                    in_=diff[b, c0][:, :, n0 : n0 + part].rearrange("p t (c i) -> p c t i", i=4),
+                    func=ACT.Abs,
+                )
+
+        def difference_on_vector(b, c0):
+            cols = slice(c0, c0 + P)
+            half = c0 // BANK
+            inner = slice(c0 % BANK, c0 % BANK + P)
+            acc = bank([P, PACK, P])
+            for t in range(PACK):
+                pass_w1(acc[:, t, :], 0, b, t, cols, True, False)
+                if (b, half, t) in FOLDED:
+                    pass_w2(acc[:, t, :], b, t, cols, False, False)
+                pass_w1(acc[:, t, :], 1, b, t, cols, False, True)
+            diff[b, c0] = ring.tile([P, P, PACK], F32, name="woven", bufs=2)
+            nc.vector.tensor_tensor(
+                out=diff[b, c0][:], in0=acc[:].rearrange("p t n -> p n t"),
+                in1=reading[b, half][:, :, inner].rearrange("p t n -> p n t"), op=ALU.subtract,
+            )
+
+        def abs_on_vector(b, c0):
+            h16[b, c0] = ring.tile([P, PACK * P], BF16, name="h16", align_bytes=64, bufs=4)
+            flat = diff[b, c0][:].rearrange("p n t -> p (n t)")
+            nc.vector.scalar_tensor_tensor(out=h16[b, c0][:], in0=flat, scalar=-1.0, in1=flat, op0=ALU.mult, op1=ALU.max)
+
+        def quantize_h(b, c0, width):
+            for n0 in range(c0, c0 + width, ABS_WIDTH):
+                cols = slice(n0, n0 + min(width, ABS_WIDTH))
+                nc.vector.quantize_mx(out=h_c[b][:, cols].bitcast(FP8X4), scales=h_s[b][:, cols], in_=h16[b, n0][:])
+
+        def scores(c0, width):
+            step = BANK if width == BANK else P
+            per_bank = BINS if width == P else 1
+            result = kept("result%d" % c0, [P, BINS, width], F32)
+            for first in range(0, BINS, per_bank):
+                acc = bank([P, per_bank, width])
+                for c in range(first, first + per_bank):
+                    for n0 in range(0, width, step):
+                        cols = slice(c0 + n0, c0 + n0 + step)
+                        for b in range(GROUPS):
+                            nc.tensor.matmul_mx(
+                                out=acc[:, c - first, n0 : n0 + step],
+                                lhsT=w4_c[:, b, 2 * c * P : 2 * (c + 1) * P].bitcast(FP4X4), lhsT_scale=w4_s[:, b, c * P : (c + 1) * P],
+                                rhs=h_c[b][:, cols].bitcast(FP8X4), rhs_scale=h_s[b][:, cols],
+                                start=(b == 0), stop=(b == GROUPS - 1),
+                            )
+                for c in range(first, first + per_bank):
+                    nc.scalar.activation(out=result[:, c, :], in_=acc[:, c - first, :], func=ACT.Sigmoid, bias=bias_c[:, c : c + 1])
+                    if width == BANK:
+                        nc.sync.dma_start(out=out[c * P : (c + 1) * P, c0 : c0 + width], in_=result[:, c, :])
+            if width < BANK:
+                nc.sync.dma_start(out=out[:, c0 : c0 + width].rearrange("(c p) n -> p c n", p=P), in_=result[:])
+
+        def gather_scales():
+            nc.vector.tensor_copy(picked_s[:], tab_s[:].indirect(offsets[:]))
+
+        def gather_words(a):
+            picked_c[a] = keep.tile([P, S], U32, name="picked_c", tag="picked_c%d" % a, align_bytes=64, bufs=1)
+            nc.vector.tensor_copy(picked_c[a][:], tab_c[a][:].indirect(offsets[:]))
+
+        tab_s = late_tile("tab_s", [P, T], U8, T)
+        w4_s = late_tile("w4_s", [P, GROUPS, N], U8, GROUPS * N)
+        w4_c = late_tile("w4_c", [P, GROUPS, 2 * N], U8, GROUPS * 2 * N)
+        bias_c = late_tile("bias_c", [P, BINS], F32, 64)
+        nc.vector.memset(tab_s[:].bitcast(I32), 0)
+        nc.vector.memset(w4_s[:].bitcast(I32), 0)
+
+        def load_table_scales():
+            for q in range(4):
+                nc.sync.dma_start(out=tab_s[32 * q : 32 * q + 8, :].bitcast(I32), in_=tab_scales[:, 4 * q : 4 * q + 4, :].bitcast(I32))
+
+        def load_w4():
+            for q in range(4):
+                nc.sync.dma_start(
+                    out=w4_s[32 * q : 32 * q + 4, :, :].bitcast(I32),
+                    in_=w4_scales[:, 4 * q : 4 * q + 4, :].rearrange("a r n -> r a n").bitcast(I32),
+                )
+            nc.sync.dma_start(out=w4_c[:].bitcast(I32), in_=w4_words.rearrange("a p n -> p a n").bitcast(I32))
+            with nc.allow_non_contiguous_dma(reason="one bias value a partition"):
+                nc.sync.dma_start(out=bias_c[:], in_=bias.rearrange("(c p) -> p c", p=P))
+
+        load_table(0)
+        load_table_scales()
+        load_late_weight(("w2", 0, 1))
+        load_late_weight(("w1", 0, 0))
+        load_table(1)
+        load_late_weight(("w1", 1, 0))
+        load_late_weight(("w1", 0, 1))
+        load_late_weight(("w1", 1, 1))
+        load_w4()
+
+        readings(0, 0)
+        readings(0, 1)
+        cast_weight(("w2", 0, 1))
+        gather_scales()
+        quantize_weight(("w2", 0, 1))
+        gather_words(0)
+        cast_weight(("w1", 0, 0))
+        readings(1, 0)
+        quantize_weight(("w1", 0, 0))
+        readings(1, 1)
+        gather_words(1)
+        cast_weight(("w1", 1, 0))
+        quantize_weight(("w1", 1, 0))
+        cast_weight(("w1", 0, 1))
+        cast_weight(("w1", 1, 1))
+        difference(0, 0, 512)
+        quantize_weight(("w1", 0, 1))
+        difference(0, 512, 512)
+        quantize_weight(("w1", 1, 1))
+        quantize_h(0, 0, 512)
+        difference(1, 0, 512)
+        quantize_h(0, 512, 512)
+        difference(1, 512, 256)
+        quantize_h(1, 0, 512)
+        difference_on_vector(1, 768)
+        scores(0, 512)
+        difference_on_vector(1, 896)
+        quantize_h(1, 512, 256)
+        abs_on_vector(1, 768)
+        abs_on_vector(1, 896)
+        scores(512, 256)
+        quantize_h(1, 768, 128)
+        quantize_h(1, 896, 128)
+        scores(768, 128)
+        scores(896, 128)

@@ -26,14 +26,14 @@ ABS_WIDTH = 256
 FOLDED = tuple((1, half, t) for half in range(2) for t in range(PACK))[:-1]
 CASTS = {
     ("w2", 0, 0): ("vector", "scalar"),
-    ("w2", 0, 1): ("scalar", "scalar"),
+    ("w2", 0, 1): ("scalar", "vector"),
     ("w1", 0, 0): ("scalar", "scalar"),
-    ("w1", 1, 0): ("scalar", "vector"),
+    ("w1", 1, 0): ("vector", "scalar"),
     ("w1", 0, 1): ("scalar", "scalar"),
-    ("w1", 1, 1): ("scalar", "scalar"),
+    ("w1", 1, 1): ("scalar", "vector"),
 }
 RAW_BYTES = PACK * KP * 4
-LATE_BYTES = 5 * RAW_BYTES + 2 * T * 4 + T + 2 * N * GROUPS + N * GROUPS + 64
+LATE_BYTES = 5 * RAW_BYTES + 2 * T * 4 + 2 * N * GROUPS + N * GROUPS + 64
 
 
 def tile_list_street_reading_mismatch_kernel(
@@ -64,9 +64,11 @@ def tile_list_street_reading_mismatch_kernel(
         offsets = keep.tile([P, S // 16], U16, name="offsets")
 
         warm_in = keep.tile([P, 8], F32, name="warm_in", tag="xs_s", align_bytes=64)
-        warm_out = keep.tile([P, 8], F32, name="warm_out", tag="xs_c", align_bytes=64)
+        warm_out = keep.tile([P, 8], F32, name="warm_out", tag="first_raw", align_bytes=64)
+        warm_bias = keep.tile([P, 8], F32, name="warm_bias", tag="tab_s", align_bytes=64)
         nc.vector.memset(warm_in[:], 0.0)
-        nc.scalar.activation(out=warm_out[:], in_=warm_in[:], func=ACT.Sigmoid)
+        nc.vector.memset(warm_bias[:], 0.0)
+        nc.scalar.activation(out=warm_out[:], in_=warm_in[:], func=ACT.Sigmoid, bias=warm_bias[:, 0:1])
 
         xs_s = keep.tile([P, S], U8, name="xs_s", tag="xs_s", align_bytes=64)
         w3_s_in = kept("w3_s_in", [P, H], U8)
@@ -77,7 +79,7 @@ def tile_list_street_reading_mismatch_kernel(
         tab_c = {}
 
         def load_weight(key, tile):
-            raw[key] = tile
+            raw[key] = tile[:].rearrange("p (j c) -> p j c", j=PACK)
             w = w1 if key[0] == "w1" else w2
             rows = w[key[1] * KP : (key[1] + 1) * KP, key[2] * KP : (key[2] + 1) * KP]
             nc.sync.dma_start(out=tile[:].rearrange("p (j c) -> p j c", j=PACK), in_=rows.rearrange("(p j) c -> p j c", j=PACK))
@@ -85,18 +87,24 @@ def tile_list_street_reading_mismatch_kernel(
         def load_late_weight(key):
             load_weight(key, late_tile("raw_%s_%d_%d" % key, [P, PACK * KP], F32, RAW_BYTES))
 
+        def load_w1_pass(a):
+            tile = late_tile("raw_w1_%d" % a, [P, PACK, H], F32, 2 * RAW_BYTES)
+            nc.sync.dma_start(out=tile[:], in_=w1[a * KP : (a + 1) * KP, :].rearrange("(p j) c -> p j c", j=PACK))
+            for b in range(GROUPS):
+                raw["w1", a, b] = tile[:, :, b * KP : (b + 1) * KP]
+
         def load_table(a):
             tab_c[a] = late_tile("tab_c%d" % a, [P, T], U32, 4 * T)
             nc.sync.dma_start(out=tab_c[a][:].bitcast(I32), in_=tab_words[a].rearrange("p n t -> p (n t)").bitcast(I32))
 
         w3_in = late.tile([P, LATE_BYTES], U8, name="w3_in", align_bytes=64, offset=0)
         nc.sync.dma_start(out=w3_in[:, : 2 * H].bitcast(I32), in_=w3_words[0].bitcast(I32))
-        load_weight(("w2", 0, 0), kept("first_raw", [P, PACK * KP], F32))
+        xs_c = kept("xs_c", [P, S], U32)
+        nc.sync.dma_start(out=xs_c[:].bitcast(I32), in_=xs_words[0].rearrange("p n t -> p (n t)").bitcast(I32))
         nc.sync.dma_start(offsets[:], offs)
         for q in range(4):
             nc.sync.dma_start(out=w3_s_in[32 * q : 32 * q + 4, :].bitcast(I32), in_=w3_scales[0, 4 * q : 4 * q + 4, :].bitcast(I32))
-        xs_c = keep.tile([P, S], U32, name="xs_c", tag="xs_c", align_bytes=64)
-        nc.sync.dma_start(out=xs_c[:].bitcast(I32), in_=xs_words[0].rearrange("p n t -> p (n t)").bitcast(I32))
+        load_weight(("w2", 0, 0), keep.tile([P, PACK * KP], F32, name="first_raw", tag="first_raw", align_bytes=64))
         for q in range(4):
             nc.sync.dma_start(out=xs_s[32 * q : 32 * q + 4, :].bitcast(I32), in_=xs_scales[0, 4 * q : 4 * q + 4, :].bitcast(I32))
 
@@ -107,12 +115,12 @@ def tile_list_street_reading_mismatch_kernel(
         def cast_weight(key):
             sign = -1.0 if key[0] == "w2" else 1.0
             for half, engine in enumerate(CASTS[key]):
-                tag = "picked_c0" if (key, half) == (("w2", 0, 1), 1) else "grouped"
-                pool = keep if tag == "picked_c0" else ring
-                tile = pool.tile([P, 2 * KP], BF16, name="grouped", tag=tag, align_bytes=64, bufs=1 if tag == "picked_c0" else 6)
+                tag = {}.get((key, half), "grouped")
+                pool = ring if tag == "grouped" else keep
+                tile = pool.tile([P, 2 * KP], BF16, name="grouped", tag=tag, align_bytes=64, bufs=6 if tag == "grouped" else 1)
                 grouped[key, half] = tile
                 order = "p m t j" if engine == "gpsimd" else "p m j t"
-                src = raw[key][:].rearrange("p (j m h t) -> h " + order, j=PACK, h=2, t=2)[half]
+                src = raw[key].rearrange("p j (m h t) -> h " + order, h=2, t=2)[half]
                 dst = tile[:].rearrange("p (t m j) -> " + order, j=PACK, t=2)
                 if engine == "scalar":
                     nc.scalar.activation(out=dst, in_=src, func=ACT.Copy, scale=sign)
@@ -196,7 +204,7 @@ def tile_list_street_reading_mismatch_kernel(
             half = c0 // BANK
             inner = slice(c0 % BANK, c0 % BANK + width)
             per_bank = BANK // width
-            diff[b, c0] = ring.tile([P, PACK, width], F32, name="diff", bufs=2)
+            diff[b, c0] = ring.tile([P, PACK, width], F32, name="diff", bufs=3)
             for t0 in range(0, PACK, per_bank):
                 acc = bank([P, per_bank, width])
                 for u in range(per_bank):
@@ -274,16 +282,17 @@ def tile_list_street_reading_mismatch_kernel(
             picked_c[a] = keep.tile([P, S], U32, name="picked_c", tag="picked_c%d" % a, align_bytes=64, bufs=1)
             nc.vector.tensor_copy(picked_c[a][:], tab_c[a][:].indirect(offsets[:]))
 
-        tab_s = late_tile("tab_s", [P, T], U8, T)
+        tab_s = keep.tile([P, T], U8, name="tab_s", tag="tab_s", align_bytes=64)
         w4_s = late_tile("w4_s", [P, GROUPS, N], U8, GROUPS * N)
         w4_c = late_tile("w4_c", [P, GROUPS, 2 * N], U8, GROUPS * 2 * N)
         bias_c = late_tile("bias_c", [P, BINS], F32, 64)
-        nc.vector.memset(tab_s[:].bitcast(I32), 0)
+        nc.gpsimd.memset(tab_s[:].bitcast(I32), 0)
         nc.vector.memset(w4_s[:].bitcast(I32), 0)
 
-        def load_table_scales():
+        def load_table_scales(a):
             for q in range(4):
-                nc.sync.dma_start(out=tab_s[32 * q : 32 * q + 8, :].bitcast(I32), in_=tab_scales[:, 4 * q : 4 * q + 4, :].bitcast(I32))
+                rows = slice(32 * q + 4 * a, 32 * q + 4 * a + 4)
+                nc.sync.dma_start(out=tab_s[rows, :].bitcast(I32), in_=tab_scales[a, 4 * q : 4 * q + 4, :].bitcast(I32))
 
         def load_w4():
             for q in range(4):
@@ -295,11 +304,12 @@ def tile_list_street_reading_mismatch_kernel(
             with nc.allow_non_contiguous_dma(reason="one bias value a partition"):
                 nc.sync.dma_start(out=bias_c[:], in_=bias.rearrange("(c p) -> p c", p=P))
 
-        load_table(0)
-        load_table_scales()
         load_late_weight(("w2", 0, 1))
-        load_late_weight(("w1", 0, 0))
+        load_table_scales(0)
+        load_table(0)
+        load_table_scales(1)
         load_table(1)
+        load_late_weight(("w1", 0, 0))
         load_late_weight(("w1", 1, 0))
         load_late_weight(("w1", 0, 1))
         load_late_weight(("w1", 1, 1))
@@ -308,30 +318,32 @@ def tile_list_street_reading_mismatch_kernel(
         readings(0, 0)
         readings(0, 1)
         cast_weight(("w2", 0, 1))
-        gather_scales()
         quantize_weight(("w2", 0, 1))
-        gather_words(0)
-        cast_weight(("w1", 0, 0))
         readings(1, 0)
-        quantize_weight(("w1", 0, 0))
         readings(1, 1)
+        gather_words(0)
+        gather_scales()
         gather_words(1)
+        cast_weight(("w1", 0, 0))
+        quantize_weight(("w1", 0, 0))
         cast_weight(("w1", 1, 0))
         quantize_weight(("w1", 1, 0))
         cast_weight(("w1", 0, 1))
-        cast_weight(("w1", 1, 1))
         difference(0, 0, 512)
         quantize_weight(("w1", 0, 1))
+        cast_weight(("w1", 1, 1))
         difference(0, 512, 512)
         quantize_weight(("w1", 1, 1))
         quantize_h(0, 0, 512)
-        difference(1, 0, 512)
+        difference(1, 0, 256)
+        difference(1, 256, 256)
         quantize_h(0, 512, 512)
+        quantize_h(1, 0, 256)
         difference(1, 512, 256)
-        quantize_h(1, 0, 512)
+        quantize_h(1, 256, 256)
         difference_on_vector(1, 768)
-        scores(0, 512)
         difference_on_vector(1, 896)
+        scores(0, 512)
         quantize_h(1, 512, 256)
         abs_on_vector(1, 768)
         abs_on_vector(1, 896)

@@ -20,20 +20,17 @@ P = 128
 PACK = 4
 KP = P * PACK
 BANK = 512
+QUARTER = 256
 GROUPS = H // KP
 BINS = N // P
-ABS_WIDTH = 256
-FOLDED = tuple((1, half, t) for half in range(2) for t in range(PACK))[:-1]
-CASTS = {
-    ("w2", 0, 0): ("vector", "scalar"),
-    ("w2", 0, 1): ("scalar", "vector"),
-    ("w1", 0, 0): ("scalar", "scalar"),
-    ("w1", 1, 0): ("vector", "scalar"),
-    ("w1", 0, 1): ("scalar", "scalar"),
-    ("w1", 1, 1): ("scalar", "vector"),
-}
 RAW_BYTES = PACK * KP * 4
-LATE_BYTES = 5 * RAW_BYTES + 2 * T * 4 + 2 * N * GROUPS + N * GROUPS + 64
+GROUPED_BYTES = 2 * KP * 2
+CODE_BYTES = 2 * P * 4
+LATE_BYTES = 5 * RAW_BYTES + 2 * T * 4 + 3 * N * GROUPS + 64
+
+
+def folded(b, half, t):
+    return b == 0 and (half, t) != (0, 0)
 
 
 def tile_list_street_reading_mismatch_kernel(
@@ -42,37 +39,55 @@ def tile_list_street_reading_mismatch_kernel(
     nc = tc.nc
     with ExitStack() as ctx:
         keep = ctx.enter_context(tc.tile_pool(name="keep", bufs=1))
-        late = ctx.enter_context(tc.tile_pool(name="late", bufs=1))
-        ring = ctx.enter_context(tc.tile_pool(name="ring", bufs=2))
+        arena = ctx.enter_context(tc.tile_pool(name="arena", bufs=1))
+        ring = ctx.enter_context(tc.tile_pool(name="ring", bufs=4))
         psum = ctx.enter_context(tc.psum_pool(name="psum", bufs=1))
         banks_used = []
-        late_used = []
+        arena_used = []
+        place = {}
 
-        def bank(shape):
-            tag = "bank%d" % (len(banks_used) % 8)
-            banks_used.append(tag)
-            return psum.tile(shape, F32, name=tag, tag=tag)
+        def bank(shape, index=None):
+            if index is None:
+                index = len(banks_used) % 8
+                banks_used.append(index)
+            return psum.tile(shape, F32, name="bank%d" % index, tag="bank%d" % index)
 
         def kept(name, shape, dtype):
             return keep.tile(shape, dtype, name=name, align_bytes=64)
 
-        def late_tile(name, shape, dtype, nbytes):
-            tile = late.tile(shape, dtype, name=name, align_bytes=64, offset=sum(late_used))
-            late_used.append(nbytes)
-            return tile
+        def reserve(name, nbytes):
+            place[name] = sum(arena_used)
+            arena_used.append(nbytes)
+
+        def placed(name, shape, dtype, on, skip=0):
+            place[name] = place[on] + skip
+            return arena.tile(shape, dtype, name=name, align_bytes=64, offset=place[name])
+
+        def fresh(name, shape, dtype, nbytes):
+            reserve(name, nbytes)
+            return placed(name, shape, dtype, name)
+
+        def load_scale_rows(plane, first, rows):
+            for r in range(4):
+                nc.sync.dma_start(out=plane[first + r : P : 32].bitcast(I32), in_=rows[r].bitcast(I32))
 
         offsets = keep.tile([P, S // 16], U16, name="offsets")
 
         warm_in = keep.tile([P, 8], F32, name="warm_in", tag="xs_s", align_bytes=64)
         warm_out = keep.tile([P, 8], F32, name="warm_out", tag="first_raw", align_bytes=64)
-        warm_bias = keep.tile([P, 8], F32, name="warm_bias", tag="tab_s", align_bytes=64)
         nc.vector.memset(warm_in[:], 0.0)
-        nc.vector.memset(warm_bias[:], 0.0)
-        nc.scalar.activation(out=warm_out[:], in_=warm_in[:], func=ACT.Sigmoid, bias=warm_bias[:, 0:1])
+        nc.scalar.activation(out=warm_out[:], in_=warm_in[:], func=ACT.Sigmoid)
 
         xs_s = keep.tile([P, S], U8, name="xs_s", tag="xs_s", align_bytes=64)
         w3_s_in = kept("w3_s_in", [P, H], U8)
+        for name, nbytes in (
+            ("raw_w2_0_0", RAW_BYTES), ("tab_c0", 4 * T), ("tab_c1", 4 * T), ("raw_w1_0_0", RAW_BYTES), ("raw_w1_1_0", RAW_BYTES),
+            ("raw_w1_0_1", RAW_BYTES), ("raw_w1_1_1", RAW_BYTES), ("w4_s", GROUPS * N), ("w4_c", 2 * GROUPS * N), ("bias_c", 64),
+        ):
+            reserve(name, nbytes)
+        tab_s = fresh("tab_s", [P, T], U8, T)
         nc.vector.memset(w3_s_in[:].bitcast(I32), 0)
+        nc.vector.memset(tab_s[:].bitcast(I32), 0)
         nc.vector.memset(xs_s[:].bitcast(I32), 0)
 
         raw = {}
@@ -82,58 +97,25 @@ def tile_list_street_reading_mismatch_kernel(
             raw[key] = tile[:].rearrange("p (j c) -> p j c", j=PACK)
             w = w1 if key[0] == "w1" else w2
             rows = w[key[1] * KP : (key[1] + 1) * KP, key[2] * KP : (key[2] + 1) * KP]
-            nc.sync.dma_start(out=tile[:].rearrange("p (j c) -> p j c", j=PACK), in_=rows.rearrange("(p j) c -> p j c", j=PACK))
+            nc.sync.dma_start(out=raw[key], in_=rows.rearrange("(p j) c -> p j c", j=PACK))
 
         def load_late_weight(key):
-            load_weight(key, late_tile("raw_%s_%d_%d" % key, [P, PACK * KP], F32, RAW_BYTES))
-
-        def load_w1_pass(a):
-            tile = late_tile("raw_w1_%d" % a, [P, PACK, H], F32, 2 * RAW_BYTES)
-            nc.sync.dma_start(out=tile[:], in_=w1[a * KP : (a + 1) * KP, :].rearrange("(p j) c -> p j c", j=PACK))
-            for b in range(GROUPS):
-                raw["w1", a, b] = tile[:, :, b * KP : (b + 1) * KP]
+            name = "raw_%s_%d_%d" % key
+            load_weight(key, placed(name, [P, PACK * KP], F32, name))
 
         def load_table(a):
-            tab_c[a] = late_tile("tab_c%d" % a, [P, T], U32, 4 * T)
+            load_scale_rows(tab_s, 4 * a, tab_scales[a].rearrange("(q r) n -> r q n", r=4))
+            tab_c[a] = placed("tab_c%d" % a, [P, T], U32, "tab_c%d" % a)
             nc.sync.dma_start(out=tab_c[a][:].bitcast(I32), in_=tab_words[a].rearrange("p n t -> p (n t)").bitcast(I32))
 
-        w3_in = late.tile([P, LATE_BYTES], U8, name="w3_in", align_bytes=64, offset=0)
+        w3_in = placed("w3_in", [P, LATE_BYTES], U8, "raw_w2_0_0")
         nc.sync.dma_start(out=w3_in[:, : 2 * H].bitcast(I32), in_=w3_words[0].bitcast(I32))
         xs_c = kept("xs_c", [P, S], U32)
         nc.sync.dma_start(out=xs_c[:].bitcast(I32), in_=xs_words[0].rearrange("p n t -> p (n t)").bitcast(I32))
         nc.sync.dma_start(offsets[:], offs)
-        for q in range(4):
-            nc.sync.dma_start(out=w3_s_in[32 * q : 32 * q + 4, :].bitcast(I32), in_=w3_scales[0, 4 * q : 4 * q + 4, :].bitcast(I32))
-        load_weight(("w2", 0, 0), keep.tile([P, PACK * KP], F32, name="first_raw", tag="first_raw", align_bytes=64))
-        for q in range(4):
-            nc.sync.dma_start(out=xs_s[32 * q : 32 * q + 4, :].bitcast(I32), in_=xs_scales[0, 4 * q : 4 * q + 4, :].bitcast(I32))
-
-        codes = {}
-        scales = {}
-        grouped = {}
-
-        def cast_weight(key):
-            sign = -1.0 if key[0] == "w2" else 1.0
-            for half, engine in enumerate(CASTS[key]):
-                tag = {}.get((key, half), "grouped")
-                pool = ring if tag == "grouped" else keep
-                tile = pool.tile([P, 2 * KP], BF16, name="grouped", tag=tag, align_bytes=64, bufs=6 if tag == "grouped" else 1)
-                grouped[key, half] = tile
-                order = "p m t j" if engine == "gpsimd" else "p m j t"
-                src = raw[key].rearrange("p j (m h t) -> h " + order, h=2, t=2)[half]
-                dst = tile[:].rearrange("p (t m j) -> " + order, j=PACK, t=2)
-                if engine == "scalar":
-                    nc.scalar.activation(out=dst, in_=src, func=ACT.Copy, scale=sign)
-                elif engine == "vector":
-                    nc.vector.tensor_scalar(out=dst, in0=src, scalar1=sign, scalar2=None, op0=ALU.mult)
-                else:
-                    nc.gpsimd.tensor_scalar(out=dst, in0=src, scalar1=sign, scalar2=0.0, op0=ALU.mult, op1=ALU.add)
-
-        def quantize_weight(key):
-            for half in range(2):
-                codes[key, half] = kept("c_%s_%d_%d" % key + "_%d" % half, [P, 2 * P], U32)
-                scales[key, half] = kept("s_%s_%d_%d" % key + "_%d" % half, [P, 2 * P], U8)
-                nc.vector.quantize_mx(out=codes[key, half][:].bitcast(FP8X4), scales=scales[key, half][:], in_=grouped[key, half][:])
+        load_scale_rows(w3_s_in, 0, w3_scales[0].rearrange("(q r) n -> r q n", r=4))
+        load_weight(("w2", 0, 1), keep.tile([P, PACK * KP], F32, name="first_raw", tag="first_raw", align_bytes=64))
+        load_scale_rows(xs_s, 0, xs_scales[0].rearrange("(q r) n -> r q n", r=4))
 
         w3_c = kept("w3_c", [P, 2 * H], U8)
         w3_s = kept("w3_s", [P, H], U8)
@@ -141,214 +123,306 @@ def tile_list_street_reading_mismatch_kernel(
             out=w3_c[:].bitcast(U16).rearrange("p (b t m) -> p b t m", b=GROUPS, t=PACK),
             in_=w3_in[:, : 2 * H].bitcast(U16).rearrange("p (b m t) -> p b t m", b=GROUPS, t=PACK),
         )
-        cast_weight(("w2", 0, 0))
         nc.vector.tensor_copy(
             out=w3_s[:].rearrange("p (b t m) -> p b t m", b=GROUPS, t=PACK),
             in_=w3_s_in[:].rearrange("p (b m t) -> p b t m", b=GROUPS, t=PACK),
         )
-        quantize_weight(("w2", 0, 0))
 
-        def pass_w2(acc, b, t, cols, start, stop):
-            key = (("w2", 0, b), t // 2)
+        w4_s = placed("w4_s", [P, GROUPS, N], U8, "w4_s")
+        w4_c = placed("w4_c", [P, GROUPS, 2 * N], U8, "w4_c")
+        bias_c = placed("bias_c", [P, BINS], F32, "bias_c")
+        nc.vector.memset(w4_s[:].bitcast(I32), 0)
+
+        load_late_weight(("w2", 0, 0))
+        load_table(0)
+        load_table(1)
+        for b in range(GROUPS):
+            for a in range(K // KP):
+                load_late_weight(("w1", a, b))
+        load_scale_rows(w4_s, 0, w4_scales.rearrange("a (q r) n -> r q a n", r=4))
+        nc.sync.dma_start(out=w4_c[:].bitcast(I32), in_=w4_words.rearrange("a p n -> p a n").bitcast(I32))
+        with nc.allow_non_contiguous_dma(reason="one bias value a partition"):
+            nc.sync.dma_start(out=bias_c[:], in_=bias.rearrange("(c p) -> p c", p=P))
+
+        codes = {}
+        scales = {}
+        grouped = {}
+
+        def cast(key, u, engine, on=None, skip=0):
+            sign = -1.0 if key[0] == "w2" else 1.0
+            name = "grouped_%s_%d_%d" % key + "_%d" % u
+            if on is None:
+                grouped[key, u] = fresh(name, [P, 2 * KP], BF16, GROUPED_BYTES)
+            else:
+                grouped[key, u] = placed(name, [P, 2 * KP], BF16, on, skip)
+            src = raw[key].rearrange("p j (m h t) -> h p m j t", h=2, t=2)[u]
+            dst = grouped[key, u][:].rearrange("p (t m j) -> p m j t", j=PACK, t=2)
+            if engine == "scalar":
+                nc.scalar.activation(out=dst, in_=src, func=ACT.Copy, scale=sign)
+            else:
+                nc.vector.tensor_scalar(out=dst, in0=src, scalar1=sign, scalar2=None, op0=ALU.mult)
+
+        def quantize(key, u, on=None, skip=0, scales_on=None, scales_skip=0):
+            name = "codes_%s_%d_%d" % key + "_%d" % u
+            if on is None:
+                codes[key, u] = fresh(name, [P, 2 * P], U32, CODE_BYTES)
+            else:
+                codes[key, u] = placed(name, [P, 2 * P], U32, on, skip)
+            name = "scales_%s_%d_%d" % key + "_%d" % u
+            if scales_on is None:
+                scales[key, u] = kept(name, [P, 2 * P], U8)
+            else:
+                scales[key, u] = placed(name, [P, 2 * P], U8, scales_on, scales_skip)
+            nc.vector.quantize_mx(out=codes[key, u][:].bitcast(FP8X4), scales=scales[key, u][:], in_=grouped[key, u][:])
+
+        picked_c = {}
+        picked_s = {}
+
+        def weight_pass(acc, key, t, cols, start, stop):
+            m = slice(t % 2 * P, (t % 2 + 1) * P)
+            if key[0] == "w2":
+                rhs, rhs_scale = xs_c[:, cols], xs_s[:, cols]
+            else:
+                rhs, rhs_scale = picked_c[key[1]][:, cols], picked_s[0][4 * key[1] : P, cols]
             nc.tensor.matmul_mx(
-                out=acc, lhsT=codes[key][:, t % 2 * P : (t % 2 + 1) * P].bitcast(FP8X4), lhsT_scale=scales[key][:, t % 2 * P : (t % 2 + 1) * P],
-                rhs=xs_c[:, cols].bitcast(FP8X4), rhs_scale=xs_s[:, cols], start=start, stop=stop,
+                out=acc, lhsT=codes[key, t // 2][:, m].bitcast(FP8X4), lhsT_scale=scales[key, t // 2][:, m],
+                rhs=rhs.bitcast(FP8X4), rhs_scale=rhs_scale, start=start, stop=stop,
             )
 
-        def pass_w3(acc, b, t, cols, start, stop):
+        def w3_pass(acc, b, t, cols, start, stop):
             m0 = b * KP + t * P
             nc.tensor.matmul_mx(
                 out=acc, lhsT=w3_c[:, 2 * m0 : 2 * (m0 + P)].bitcast(FP4X4), lhsT_scale=w3_s[:, m0 : m0 + P],
                 rhs=xs_c[:, cols].bitcast(FP8X4), rhs_scale=xs_s[:, cols], start=start, stop=stop,
             )
 
-        picked_c = {}
-        picked_s = kept("picked_s", [P, S], U8)
+        reading = {}
+        read2 = {}
+        for b in range(GROUPS):
+            for half in range(2):
+                for u in range(2):
+                    if (b, u) == (1, 0):
+                        reserve("reading1%d" % half, 4 * PACK * BANK)
+                    elif b == 0:
+                        reserve("reading0%d%d" % (half, u), 4 * 2 * BANK)
 
-        def pass_w1(acc, a, b, t, cols, start, stop):
-            key = (("w1", a, b), t // 2)
-            nc.tensor.matmul_mx(
-                out=acc, lhsT=codes[key][:, t % 2 * P : (t % 2 + 1) * P].bitcast(FP8X4), lhsT_scale=scales[key][:, t % 2 * P : (t % 2 + 1) * P],
-                rhs=picked_c[a][:, cols].bitcast(FP8X4), rhs_scale=picked_s[4 * a : P, cols], start=start, stop=stop,
+        def reading_slot(b, half, t):
+            if b == 0:
+                name, key, shape, row = "reading0%d%d" % (half, t // 2), (0, half, t // 2), [P, 2, BANK], t % 2
+            else:
+                name, key, shape, row = "reading1%d" % half, (1, half), [P, PACK, BANK], t
+            if key not in reading:
+                reading[key] = placed(name, shape, F32, name)
+            return reading[key][:, row, :]
+
+        def second_reading(b, half, t, on=None, skip=0):
+            acc = bank([P, BANK])
+            w3_pass(acc[:], b, t, slice(half * BANK, (half + 1) * BANK), True, True)
+            name = "read2_%d%d%d" % (b, half, t)
+            if on is None:
+                read2[b, half, t] = fresh(name, [P, BANK], F32, 4 * BANK)
+            else:
+                read2[b, half, t] = placed(name, [P, BANK], F32, on, skip)
+            nc.scalar.copy(out=read2[b, half, t][:], in_=acc[:])
+
+        def larger_reading(b, half, t):
+            acc = bank([P, BANK])
+            weight_pass(acc[:], ("w2", 0, b), t, slice(half * BANK, (half + 1) * BANK), True, True)
+            nc.vector.scalar_tensor_tensor(
+                out=reading_slot(b, half, t), in0=acc[:], scalar=-1.0, in1=read2[b, half, t][:], op0=ALU.mult, op1=ALU.max
             )
 
-        reading = {}
-
-        def readings(b, half):
+        def excess_reading(b, half, t):
+            acc = bank([P, BANK])
             cols = slice(half * BANK, (half + 1) * BANK)
-            reading[b, half] = kept("reading%d%d" % (b, half), [P, PACK, BANK], F32)
-            for t in range(PACK):
-                if (b, half, t) in FOLDED:
-                    acc = bank([P, BANK])
-                    pass_w3(acc[:], b, t, cols, True, False)
-                    pass_w2(acc[:], b, t, cols, False, True)
-                    nc.scalar.activation(out=reading[b, half][:, t, :], in_=acc[:], func=ACT.Relu)
-                else:
-                    acc2 = bank([P, BANK])
-                    pass_w3(acc2[:], b, t, cols, True, True)
-                    read2 = ring.tile([P, BANK], F32, name="read2", bufs=4)
-                    nc.scalar.copy(out=read2[:], in_=acc2[:])
-                    acc1 = bank([P, BANK])
-                    pass_w2(acc1[:], b, t, cols, True, True)
-                    nc.vector.scalar_tensor_tensor(
-                        out=reading[b, half][:, t, :], in0=acc1[:], scalar=-1.0, in1=read2[:], op0=ALU.mult, op1=ALU.max
-                    )
+            w3_pass(acc[:], b, t, cols, True, False)
+            weight_pass(acc[:], ("w2", 0, b), t, cols, False, True)
+            nc.scalar.activation(out=reading_slot(b, half, t), in_=acc[:], func=ACT.Relu)
 
         h_c = [kept("h_c%d" % b, [P, S], U32) for b in range(GROUPS)]
         h_s = [kept("h_s%d" % b, [P, S], U8) for b in range(GROUPS)]
+        names = {}
         diff = {}
         h16 = {}
 
-        def difference(b, c0, width):
+        def name_passes(b, c0, width, ts, index, keys):
             cols = slice(c0, c0 + width)
-            half = c0 // BANK
-            inner = slice(c0 % BANK, c0 % BANK + width)
-            per_bank = BANK // width
-            diff[b, c0] = ring.tile([P, PACK, width], F32, name="diff", bufs=3)
-            for t0 in range(0, PACK, per_bank):
-                acc = bank([P, per_bank, width])
-                for u in range(per_bank):
-                    t = t0 + u
-                    pass_w1(acc[:, u, :], 0, b, t, cols, True, False)
-                    if (b, half, t) in FOLDED:
-                        pass_w2(acc[:, u, :], b, t, cols, False, False)
-                    pass_w1(acc[:, u, :], 1, b, t, cols, False, True)
-                nc.vector.tensor_tensor(
-                    out=diff[b, c0][:, t0 : t0 + per_bank, :], in0=acc[:],
-                    in1=reading[b, half][:, t0 : t0 + per_bank, inner], op=ALU.subtract,
-                )
-            for n0 in range(0, width, ABS_WIDTH):
-                part = min(width, ABS_WIDTH)
-                h16[b, c0 + n0] = ring.tile([P, PACK * part], BF16, name="h16", align_bytes=64, bufs=4)
-                nc.scalar.activation(
-                    out=h16[b, c0 + n0][:].rearrange("p (c i t) -> p c t i", i=4, t=PACK),
-                    in_=diff[b, c0][:, :, n0 : n0 + part].rearrange("p t (c i) -> p c t i", i=4),
-                    func=ACT.Abs,
-                )
+            if (b, c0, ts) not in names:
+                todo = [
+                    (key, t) for key in (("w2", 0, b), ("w1", 0, b), ("w1", 1, b)) for t in ts
+                    if key[0] == "w1" or folded(b, c0 // BANK, t)
+                ]
+                names[b, c0, ts] = (bank([P, len(ts), width], index), todo)
+            acc, todo = names[b, c0, ts]
+            for key, t in todo:
+                if key in keys:
+                    weight_pass(acc[:, t - ts[0], :], key, t, cols, (key, t) == todo[0], (key, t) == todo[-1])
 
-        def difference_on_vector(b, c0):
-            cols = slice(c0, c0 + P)
-            half = c0 // BANK
-            inner = slice(c0 % BANK, c0 % BANK + P)
-            acc = bank([P, PACK, P])
-            for t in range(PACK):
-                pass_w1(acc[:, t, :], 0, b, t, cols, True, False)
-                if (b, half, t) in FOLDED:
-                    pass_w2(acc[:, t, :], b, t, cols, False, False)
-                pass_w1(acc[:, t, :], 1, b, t, cols, False, True)
-            diff[b, c0] = ring.tile([P, P, PACK], F32, name="woven", bufs=2)
+        def quarter_passes(b, q, u, keys):
+            name_passes(b, q * QUARTER, QUARTER, (2 * u, 2 * u + 1), 2 * q + u, keys)
+
+        def subtract(b, q, u):
+            if (b, q) not in diff:
+                diff[b, q] = ring.tile([P, PACK, QUARTER], F32, name="diff")
+            inner = slice(q % 2 * QUARTER, (q % 2 + 1) * QUARTER)
+            if b == 0:
+                known = reading[0, q // 2, u][:, :, inner]
+            else:
+                known = reading[1, q // 2][:, 2 * u : 2 * u + 2, inner]
             nc.vector.tensor_tensor(
-                out=diff[b, c0][:], in0=acc[:].rearrange("p t n -> p n t"),
-                in1=reading[b, half][:, :, inner].rearrange("p t n -> p n t"), op=ALU.subtract,
+                out=diff[b, q][:, 2 * u : 2 * u + 2, :], in0=names[b, q * QUARTER, (2 * u, 2 * u + 1)][0][:], in1=known, op=ALU.subtract
+            )
+
+        def abs_on_scalar(b, q):
+            h16[b, q * QUARTER] = ring.tile([P, PACK * QUARTER], BF16, name="h16", align_bytes=64)
+            nc.scalar.activation(
+                out=h16[b, q * QUARTER][:].rearrange("p (c i t) -> p c t i", i=4, t=PACK),
+                in_=diff[b, q][:].rearrange("p t (c i) -> p c t i", i=4),
+                func=ACT.Abs,
+            )
+
+        woven = {}
+
+        def subtract_woven(b, c0):
+            inner = slice(c0 % BANK, c0 % BANK + P)
+            woven[c0] = ring.tile([P, P, PACK], F32, name="woven", bufs=2)
+            nc.vector.tensor_tensor(
+                out=woven[c0][:], in0=names[b, c0, (0, 1, 2, 3)][0][:].rearrange("p t n -> p n t"),
+                in1=reading[b, c0 // BANK][:, :, inner].rearrange("p t n -> p n t"), op=ALU.subtract,
             )
 
         def abs_on_vector(b, c0):
-            h16[b, c0] = ring.tile([P, PACK * P], BF16, name="h16", align_bytes=64, bufs=4)
-            flat = diff[b, c0][:].rearrange("p n t -> p (n t)")
+            h16[b, c0] = ring.tile([P, PACK * P], BF16, name="h16_last", align_bytes=64, bufs=2)
+            flat = woven[c0][:].rearrange("p n t -> p (n t)")
             nc.vector.scalar_tensor_tensor(out=h16[b, c0][:], in0=flat, scalar=-1.0, in1=flat, op0=ALU.mult, op1=ALU.max)
 
         def quantize_h(b, c0, width):
-            for n0 in range(c0, c0 + width, ABS_WIDTH):
-                cols = slice(n0, n0 + min(width, ABS_WIDTH))
-                nc.vector.quantize_mx(out=h_c[b][:, cols].bitcast(FP8X4), scales=h_s[b][:, cols], in_=h16[b, n0][:])
+            cols = slice(c0, c0 + width)
+            nc.vector.quantize_mx(out=h_c[b][:, cols].bitcast(FP8X4), scales=h_s[b][:, cols], in_=h16[b, c0][:])
 
-        def scores(c0, width):
-            step = BANK if width == BANK else P
-            per_bank = BINS if width == P else 1
+        def scores(c0, width, indices, store_each=False):
+            per_bank = min(BINS, BANK // width)
             result = kept("result%d" % c0, [P, BINS, width], F32)
-            for first in range(0, BINS, per_bank):
-                acc = bank([P, per_bank, width])
-                for c in range(first, first + per_bank):
-                    for n0 in range(0, width, step):
-                        cols = slice(c0 + n0, c0 + n0 + step)
-                        for b in range(GROUPS):
-                            nc.tensor.matmul_mx(
-                                out=acc[:, c - first, n0 : n0 + step],
-                                lhsT=w4_c[:, b, 2 * c * P : 2 * (c + 1) * P].bitcast(FP4X4), lhsT_scale=w4_s[:, b, c * P : (c + 1) * P],
-                                rhs=h_c[b][:, cols].bitcast(FP8X4), rhs_scale=h_s[b][:, cols],
-                                start=(b == 0), stop=(b == GROUPS - 1),
-                            )
-                for c in range(first, first + per_bank):
+            for first, index in zip(range(0, BINS, per_bank), indices):
+                bins = range(first, min(first + per_bank, BINS))
+                acc = bank([P, len(bins), width], index)
+                todo = [(b, c, n0) for b in range(GROUPS) for c in bins for n0 in range(0, width, P)]
+                for b, c, n0 in todo:
+                    cols = slice(c0 + n0, c0 + n0 + P)
+                    nc.tensor.matmul_mx(
+                        out=acc[:, c - first, n0 : n0 + P],
+                        lhsT=w4_c[:, b, 2 * c * P : 2 * (c + 1) * P].bitcast(FP4X4), lhsT_scale=w4_s[:, b, c * P : (c + 1) * P],
+                        rhs=h_c[b][:, cols].bitcast(FP8X4), rhs_scale=h_s[b][:, cols],
+                        start=(b, c, n0) == todo[0], stop=(b, c, n0) == todo[-1],
+                    )
+                for c in bins:
                     nc.scalar.activation(out=result[:, c, :], in_=acc[:, c - first, :], func=ACT.Sigmoid, bias=bias_c[:, c : c + 1])
-                    if width == BANK:
+                    if store_each:
                         nc.sync.dma_start(out=out[c * P : (c + 1) * P, c0 : c0 + width], in_=result[:, c, :])
-            if width < BANK:
+            if not store_each:
                 nc.sync.dma_start(out=out[:, c0 : c0 + width].rearrange("(c p) n -> p c n", p=P), in_=result[:])
 
-        def gather_scales():
-            nc.vector.tensor_copy(picked_s[:], tab_s[:].indirect(offsets[:]))
-
-        def gather_words(a):
-            picked_c[a] = keep.tile([P, S], U32, name="picked_c", tag="picked_c%d" % a, align_bytes=64, bufs=1)
+        def gather_words(a, on):
+            picked_c[a] = placed("picked_c%d" % a, [P, S], U32, on)
             nc.vector.tensor_copy(picked_c[a][:], tab_c[a][:].indirect(offsets[:]))
 
-        tab_s = keep.tile([P, T], U8, name="tab_s", tag="tab_s", align_bytes=64)
-        w4_s = late_tile("w4_s", [P, GROUPS, N], U8, GROUPS * N)
-        w4_c = late_tile("w4_c", [P, GROUPS, 2 * N], U8, GROUPS * 2 * N)
-        bias_c = late_tile("bias_c", [P, BINS], F32, 64)
-        nc.gpsimd.memset(tab_s[:].bitcast(I32), 0)
-        nc.vector.memset(w4_s[:].bitcast(I32), 0)
+        def gather_scales(on):
+            picked_s[0] = placed("picked_s", [P, S], U8, on)
+            nc.vector.tensor_copy(picked_s[0][:], tab_s[:].indirect(offsets[:]))
 
-        def load_table_scales(a):
-            for q in range(4):
-                rows = slice(32 * q + 4 * a, 32 * q + 4 * a + 4)
-                nc.sync.dma_start(out=tab_s[rows, :].bitcast(I32), in_=tab_scales[a, 4 * q : 4 * q + 4, :].bitcast(I32))
+        W20, W21 = ("w2", 0, 0), ("w2", 0, 1)
+        W00, W10, W01, W11 = ("w1", 0, 0), ("w1", 1, 0), ("w1", 0, 1), ("w1", 1, 1)
+        tiles = [(half, t) for half in range(2) for t in range(PACK)]
 
-        def load_w4():
-            for q in range(4):
-                nc.sync.dma_start(
-                    out=w4_s[32 * q : 32 * q + 4, :, :].bitcast(I32),
-                    in_=w4_scales[:, 4 * q : 4 * q + 4, :].rearrange("a r n -> r a n").bitcast(I32),
-                )
-            nc.sync.dma_start(out=w4_c[:].bitcast(I32), in_=w4_words.rearrange("a p n -> p a n").bitcast(I32))
-            with nc.allow_non_contiguous_dma(reason="one bias value a partition"):
-                nc.sync.dma_start(out=bias_c[:], in_=bias.rearrange("(c p) -> p c", p=P))
+        cast(W21, 0, "vector")
+        cast(W21, 1, "scalar")
+        quantize(W21, 0)
+        quantize(W21, 1)
+        reserve("first_pick", 4 * S)
+        reserve("gates", 3 * GROUPED_BYTES)
+        second_reading(1, *tiles[0])
+        second_reading(1, *tiles[1])
+        for i, tile in enumerate(tiles):
+            larger_reading(1, *tile)
+            if i + 2 < len(tiles):
+                second_reading(1, *tiles[i + 2], "first_pick" if i + 2 == 7 else None)
+            if i == 1:
+                cast(W20, 1, "scalar", "read2_100")
+            if i == 3:
+                cast(W20, 0, "vector", "read2_102")
+            if i == 4:
+                quantize(W20, 1, "gates", CODE_BYTES, "gates", 2 * GROUPED_BYTES)
+                quantize(W20, 0)
+        second_reading(0, 0, 0)
+        larger_reading(0, 0, 0)
+        for tile in tiles[1:]:
+            excess_reading(0, *tile)
+        gather_words(0, "first_pick")
+        gather_scales("tab_c0")
+        gather_words(1, "tab_s")
+        for q in range(4):
+            for u in range(2):
+                quarter_passes(0, q, u, (W20,))
 
-        load_late_weight(("w2", 0, 1))
-        load_table_scales(0)
-        load_table(0)
-        load_table_scales(1)
-        load_table(1)
-        load_late_weight(("w1", 0, 0))
-        load_late_weight(("w1", 1, 0))
-        load_late_weight(("w1", 0, 1))
-        load_late_weight(("w1", 1, 1))
-        load_w4()
+        cast(W00, 0, "scalar", "codes_w2_0_0_1")
+        cast(W00, 1, "scalar", "scales_w2_0_0_1")
+        quantize(W00, 0, "tab_c1")
+        cast(W10, 0, "vector", "grouped_w1_0_0_0", -CODE_BYTES)
+        cast(W10, 1, "scalar", "grouped_w1_0_0_0", CODE_BYTES)
+        quantize(W00, 1)
+        quantize(W10, 0)
+        quantize(W10, 1, "grouped_w1_1_0_0")
+        for q in range(4):
+            for u in range(2):
+                quarter_passes(0, q, u, (W00, W10))
+        cast(W01, 0, "scalar", "raw_w1_1_0", 2 * GROUPED_BYTES)
+        cast(W01, 1, "scalar", "raw_w1_1_0")
+        cast(W11, 1, "scalar", "raw_w1_0_1")
+        for q in range(2):
+            for u in range(2):
+                subtract(0, q, u)
+            abs_on_scalar(0, q)
+        quantize(W01, 0, "reading000")
+        subtract(0, 2, 0)
+        cast(W11, 0, "vector", "grouped_w1_0_1_0", -CODE_BYTES)
+        quantize(W01, 1, "grouped_w1_0_1_0", CODE_BYTES)
+        subtract(0, 2, 1)
+        abs_on_scalar(0, 2)
+        quantize(W11, 0)
+        quantize(W11, 1, "grouped_w1_0_1_1")
 
-        readings(0, 0)
-        readings(0, 1)
-        cast_weight(("w2", 0, 1))
-        quantize_weight(("w2", 0, 1))
-        readings(1, 0)
-        readings(1, 1)
-        gather_words(0)
-        gather_scales()
-        gather_words(1)
-        cast_weight(("w1", 0, 0))
-        quantize_weight(("w1", 0, 0))
-        cast_weight(("w1", 1, 0))
-        quantize_weight(("w1", 1, 0))
-        cast_weight(("w1", 0, 1))
-        difference(0, 0, 512)
-        quantize_weight(("w1", 0, 1))
-        cast_weight(("w1", 1, 1))
-        difference(0, 512, 512)
-        quantize_weight(("w1", 1, 1))
-        quantize_h(0, 0, 512)
-        difference(1, 0, 256)
-        difference(1, 256, 256)
-        quantize_h(0, 512, 512)
-        quantize_h(1, 0, 256)
-        difference(1, 512, 256)
-        quantize_h(1, 256, 256)
-        difference_on_vector(1, 768)
-        difference_on_vector(1, 896)
-        scores(0, 512)
-        quantize_h(1, 512, 256)
+        for q in range(3):
+            for u in range(2):
+                quarter_passes(1, q, u, (W01, W11))
+        subtract(0, 3, 0)
+        subtract(1, 0, 0)
+        quantize_h(0, 0, QUARTER)
+        subtract(1, 0, 1)
+        abs_on_scalar(1, 0)
+        subtract(1, 1, 0)
+        quantize_h(0, 256, QUARTER)
+        subtract(1, 1, 1)
+        abs_on_scalar(1, 1)
+        subtract(0, 3, 1)
+        quantize_h(0, 512, QUARTER)
+        name_passes(1, 768, P, (0, 1, 2, 3), 6, (W01, W11))
+        name_passes(1, 896, P, (0, 1, 2, 3), 7, (W01, W11))
+        abs_on_scalar(0, 3)
+        quantize_h(1, 0, QUARTER)
+        scores(0, QUARTER, (0, 1))
+        subtract(1, 2, 0)
+        quantize_h(1, 256, QUARTER)
+        subtract(1, 2, 1)
+        abs_on_scalar(1, 2)
+        scores(256, QUARTER, (2, 3), True)
+        subtract_woven(1, 768)
+        quantize_h(0, 768, QUARTER)
+        subtract_woven(1, 896)
         abs_on_vector(1, 768)
         abs_on_vector(1, 896)
-        scores(512, 256)
-        quantize_h(1, 768, 128)
-        quantize_h(1, 896, 128)
-        scores(768, 128)
-        scores(896, 128)
+        quantize_h(1, 768, P)
+        scores(768, P, (6,))
+        quantize_h(1, 512, QUARTER)
+        quantize_h(1, 896, P)
+        scores(512, QUARTER, (4, 5), True)
+        scores(896, P, (7,))

from contextlib import ExitStack

import concourse.mybir as mybir

K, K2, H, N, T, S = 1024, 512, 1024, 384, 4096, 1024
FLOPS = 2 * S * (K * H + 2 * K2 * H + H * N)

F32 = mybir.dt.float32
BF16 = mybir.dt.bfloat16
I32 = mybir.dt.int32
U32 = mybir.dt.uint32
U16 = mybir.dt.uint16
U8 = mybir.dt.uint8
FP8X4 = mybir.dt.float8_e4m3fn_x4
FP4X4 = mybir.dt.float4_e2m1fn_x4
ALU = mybir.AluOpType
ACT = mybir.ActivationFunctionType

P = 128
PACK = 4
KP = P * PACK
BANK = 512
QUARTER = 256
GROUPS = H // KP
BINS = N // P
RAW_BYTES = PACK * KP * 4
GROUPED_BYTES = 2 * KP * 2
CODE_BYTES = 2 * P * 4
LATE_BYTES = 5 * RAW_BYTES + 2 * T * 4 + 3 * N * GROUPS + 64


def folded(b, half, t):
    return b == 0 and (half, t) != (0, 0)


def tile_list_street_reading_mismatch_kernel(
    tc, tab_words, tab_scales, offs, xs_words, xs_scales, w1, w2, w3_words, w3_scales, w4_words, w4_scales, bias, out
):
    nc = tc.nc
    with ExitStack() as ctx:
        keep = ctx.enter_context(tc.tile_pool(name="keep", bufs=1))
        arena = ctx.enter_context(tc.tile_pool(name="arena", bufs=1))
        ring = ctx.enter_context(tc.tile_pool(name="ring", bufs=4))
        psum = ctx.enter_context(tc.psum_pool(name="psum", bufs=1))
        banks_used = []
        arena_used = []
        place = {}

        def bank(shape, index=None):
            if index is None:
                index = len(banks_used) % 8
                banks_used.append(index)
            return psum.tile(shape, F32, name="bank%d" % index, tag="bank%d" % index)

        def kept(name, shape, dtype):
            return keep.tile(shape, dtype, name=name, align_bytes=64)

        def reserve(name, nbytes):
            place[name] = sum(arena_used)
            arena_used.append(nbytes)

        def placed(name, shape, dtype, on, skip=0):
            place[name] = place[on] + skip
            return arena.tile(shape, dtype, name=name, align_bytes=64, offset=place[name])

        def fresh(name, shape, dtype, nbytes):
            reserve(name, nbytes)
            return placed(name, shape, dtype, name)

        def load_scale_rows(plane, first, rows):
            for r in range(4):
                nc.sync.dma_start(out=plane[first + r : P : 32].bitcast(I32), in_=rows[r].bitcast(I32))

        offsets = keep.tile([P, S // 16], U16, name="offsets")

        warm_in = keep.tile([P, 8], F32, name="warm_in", tag="xs_s", align_bytes=64)
        warm_out = keep.tile([P, 8], F32, name="warm_out", tag="first_raw", align_bytes=64)
        nc.vector.memset(warm_in[:], 0.0)
        nc.scalar.activation(out=warm_out[:], in_=warm_in[:], func=ACT.Sigmoid)

        xs_s = keep.tile([P, S], U8, name="xs_s", tag="xs_s", align_bytes=64)
        w3_s_in = kept("w3_s_in", [P, H], U8)
        for name, nbytes in (
            ("raw_w2_0_0", RAW_BYTES), ("tab_c0", 4 * T), ("tab_c1", 4 * T), ("raw_w1_0_0", RAW_BYTES), ("raw_w1_1_0", RAW_BYTES),
            ("raw_w1_0_1", RAW_BYTES), ("raw_w1_1_1", RAW_BYTES), ("w4_s", GROUPS * N), ("w4_c", 2 * GROUPS * N), ("bias_c", 64),
        ):
            reserve(name, nbytes)
        tab_s = fresh("tab_s", [P, T], U8, T)
        nc.vector.memset(w3_s_in[:].bitcast(I32), 0)
        nc.vector.memset(tab_s[:].bitcast(I32), 0)
        nc.vector.memset(xs_s[:].bitcast(I32), 0)

        raw = {}
        tab_c = {}

        def load_weight(key, tile):
            raw[key] = tile[:].rearrange("p (j c) -> p j c", j=PACK)
            w = w1 if key[0] == "w1" else w2
            rows = w[key[1] * KP : (key[1] + 1) * KP, key[2] * KP : (key[2] + 1) * KP]
            nc.sync.dma_start(out=raw[key], in_=rows.rearrange("(p j) c -> p j c", j=PACK))

        def load_late_weight(key):
            name = "raw_%s_%d_%d" % key
            load_weight(key, placed(name, [P, PACK * KP], F32, name))

        def load_table(a):
            load_scale_rows(tab_s, 4 * a, tab_scales[a].rearrange("(q r) n -> r q n", r=4))
            tab_c[a] = placed("tab_c%d" % a, [P, T], U32, "tab_c%d" % a)
            nc.sync.dma_start(out=tab_c[a][:].bitcast(I32), in_=tab_words[a].rearrange("p n t -> p (n t)").bitcast(I32))

        w3_in = placed("w3_in", [P, LATE_BYTES], U8, "raw_w2_0_0")
        nc.sync.dma_start(out=w3_in[:, : 2 * H].bitcast(I32), in_=w3_words[0].bitcast(I32))
        xs_c = kept("xs_c", [P, S], U32)
        nc.sync.dma_start(out=xs_c[:].bitcast(I32), in_=xs_words[0].rearrange("p n t -> p (n t)").bitcast(I32))
        nc.sync.dma_start(offsets[:], offs)
        load_scale_rows(w3_s_in, 0, w3_scales[0].rearrange("(q r) n -> r q n", r=4))
        load_weight(("w2", 0, 1), keep.tile([P, PACK * KP], F32, name="first_raw", tag="first_raw", align_bytes=64))
        load_scale_rows(xs_s, 0, xs_scales[0].rearrange("(q r) n -> r q n", r=4))

        w3_c = kept("w3_c", [P, 2 * H], U8)
        w3_s = kept("w3_s", [P, H], U8)
        nc.vector.tensor_copy(
            out=w3_c[:].bitcast(U16).rearrange("p (b t m) -> p b t m", b=GROUPS, t=PACK),
            in_=w3_in[:, : 2 * H].bitcast(U16).rearrange("p (b m t) -> p b t m", b=GROUPS, t=PACK),
        )
        nc.vector.tensor_copy(
            out=w3_s[:].rearrange("p (b t m) -> p b t m", b=GROUPS, t=PACK),
            in_=w3_s_in[:].rearrange("p (b m t) -> p b t m", b=GROUPS, t=PACK),
        )

        w4_s = placed("w4_s", [P, GROUPS, N], U8, "w4_s")
        w4_c = placed("w4_c", [P, GROUPS, 2 * N], U8, "w4_c")
        bias_c = placed("bias_c", [P, BINS], F32, "bias_c")
        nc.vector.memset(w4_s[:].bitcast(I32), 0)

        load_late_weight(("w2", 0, 0))
        load_table(0)
        load_table(1)
        for b in range(GROUPS):
            for a in range(K // KP):
                load_late_weight(("w1", a, b))
        load_scale_rows(w4_s, 0, w4_scales.rearrange("a (q r) n -> r q a n", r=4))
        nc.sync.dma_start(out=w4_c[:].bitcast(I32), in_=w4_words.rearrange("a p n -> p a n").bitcast(I32))
        with nc.allow_non_contiguous_dma(reason="one bias value a partition"):
            nc.sync.dma_start(out=bias_c[:], in_=bias.rearrange("(c p) -> p c", p=P))

        codes = {}
        scales = {}
        grouped = {}

        def cast(key, u, engine, on=None, skip=0):
            sign = -1.0 if key[0] == "w2" else 1.0
            name = "grouped_%s_%d_%d" % key + "_%d" % u
            if on is None:
                grouped[key, u] = fresh(name, [P, 2 * KP], BF16, GROUPED_BYTES)
            else:
                grouped[key, u] = placed(name, [P, 2 * KP], BF16, on, skip)
            src = raw[key].rearrange("p j (m h t) -> h p m j t", h=2, t=2)[u]
            dst = grouped[key, u][:].rearrange("p (t m j) -> p m j t", j=PACK, t=2)
            if engine == "scalar":
                nc.scalar.activation(out=dst, in_=src, func=ACT.Copy, scale=sign)
            else:
                nc.vector.tensor_scalar(out=dst, in0=src, scalar1=sign, scalar2=None, op0=ALU.mult)

        def quantize(key, u, on=None, skip=0, scales_on=None, scales_skip=0):
            name = "codes_%s_%d_%d" % key + "_%d" % u
            if on is None:
                codes[key, u] = fresh(name, [P, 2 * P], U32, CODE_BYTES)
            else:
                codes[key, u] = placed(name, [P, 2 * P], U32, on, skip)
            name = "scales_%s_%d_%d" % key + "_%d" % u
            if scales_on is None:
                scales[key, u] = kept(name, [P, 2 * P], U8)
            else:
                scales[key, u] = placed(name, [P, 2 * P], U8, scales_on, scales_skip)
            nc.vector.quantize_mx(out=codes[key, u][:].bitcast(FP8X4), scales=scales[key, u][:], in_=grouped[key, u][:])

        picked_c = {}
        picked_s = {}

        def weight_pass(acc, key, t, cols, start, stop):
            m = slice(t % 2 * P, (t % 2 + 1) * P)
            if key[0] == "w2":
                rhs, rhs_scale = xs_c[:, cols], xs_s[:, cols]
            else:
                rhs, rhs_scale = picked_c[key[1]][:, cols], picked_s[0][4 * key[1] : P, cols]
            nc.tensor.matmul_mx(
                out=acc, lhsT=codes[key, t // 2][:, m].bitcast(FP8X4), lhsT_scale=scales[key, t // 2][:, m],
                rhs=rhs.bitcast(FP8X4), rhs_scale=rhs_scale, start=start, stop=stop,
            )

        def w3_pass(acc, b, t, cols, start, stop):
            m0 = b * KP + t * P
            nc.tensor.matmul_mx(
                out=acc, lhsT=w3_c[:, 2 * m0 : 2 * (m0 + P)].bitcast(FP4X4), lhsT_scale=w3_s[:, m0 : m0 + P],
                rhs=xs_c[:, cols].bitcast(FP8X4), rhs_scale=xs_s[:, cols], start=start, stop=stop,
            )

        reading = {}
        read2 = {}
        for b in range(GROUPS):
            for half in range(2):
                for u in range(2):
                    if (b, u) == (1, 0):
                        reserve("reading1%d" % half, 4 * PACK * BANK)
                    elif b == 0:
                        reserve("reading0%d%d" % (half, u), 4 * 2 * BANK)

        def reading_slot(b, half, t):
            if b == 0:
                name, key, shape, row = "reading0%d%d" % (half, t // 2), (0, half, t // 2), [P, 2, BANK], t % 2
            else:
                name, key, shape, row = "reading1%d" % half, (1, half), [P, PACK, BANK], t
            if key not in reading:
                reading[key] = placed(name, shape, F32, name)
            return reading[key][:, row, :]

        def second_reading(b, half, t, on=None, skip=0):
            acc = bank([P, BANK])
            w3_pass(acc[:], b, t, slice(half * BANK, (half + 1) * BANK), True, True)
            name = "read2_%d%d%d" % (b, half, t)
            if on is None:
                read2[b, half, t] = fresh(name, [P, BANK], F32, 4 * BANK)
            else:
                read2[b, half, t] = placed(name, [P, BANK], F32, on, skip)
            nc.scalar.copy(out=read2[b, half, t][:], in_=acc[:])

        def larger_reading(b, half, t):
            acc = bank([P, BANK])
            weight_pass(acc[:], ("w2", 0, b), t, slice(half * BANK, (half + 1) * BANK), True, True)
            nc.vector.scalar_tensor_tensor(
                out=reading_slot(b, half, t), in0=acc[:], scalar=-1.0, in1=read2[b, half, t][:], op0=ALU.mult, op1=ALU.max
            )

        def excess_reading(b, half, t):
            acc = bank([P, BANK])
            cols = slice(half * BANK, (half + 1) * BANK)
            w3_pass(acc[:], b, t, cols, True, False)
            weight_pass(acc[:], ("w2", 0, b), t, cols, False, True)
            nc.scalar.activation(out=reading_slot(b, half, t), in_=acc[:], func=ACT.Relu)

        h_c = [kept("h_c%d" % b, [P, S], U32) for b in range(GROUPS)]
        h_s = [kept("h_s%d" % b, [P, S], U8) for b in range(GROUPS)]
        names = {}
        diff = {}
        h16 = {}

        def name_passes(b, c0, width, ts, index, keys):
            cols = slice(c0, c0 + width)
            if (b, c0, ts) not in names:
                todo = [
                    (key, t) for key in (("w2", 0, b), ("w1", 0, b), ("w1", 1, b)) for t in ts
                    if key[0] == "w1" or folded(b, c0 // BANK, t)
                ]
                names[b, c0, ts] = (bank([P, len(ts), width], index), todo)
            acc, todo = names[b, c0, ts]
            for key, t in todo:
                if key in keys:
                    weight_pass(acc[:, t - ts[0], :], key, t, cols, (key, t) == todo[0], (key, t) == todo[-1])

        def quarter_passes(b, q, u, keys):
            name_passes(b, q * QUARTER, QUARTER, (2 * u, 2 * u + 1), 2 * q + u, keys)

        def subtract(b, q, u):
            if (b, q) not in diff:
                diff[b, q] = ring.tile([P, PACK, QUARTER], F32, name="diff")
            inner = slice(q % 2 * QUARTER, (q % 2 + 1) * QUARTER)
            if b == 0:
                known = reading[0, q // 2, u][:, :, inner]
            else:
                known = reading[1, q // 2][:, 2 * u : 2 * u + 2, inner]
            nc.vector.tensor_tensor(
                out=diff[b, q][:, 2 * u : 2 * u + 2, :], in0=names[b, q * QUARTER, (2 * u, 2 * u + 1)][0][:], in1=known, op=ALU.subtract
            )

        def abs_on_scalar(b, q):
            h16[b, q * QUARTER] = ring.tile([P, PACK * QUARTER], BF16, name="h16", align_bytes=64)
            nc.scalar.activation(
                out=h16[b, q * QUARTER][:].rearrange("p (c i t) -> p c t i", i=4, t=PACK),
                in_=diff[b, q][:].rearrange("p t (c i) -> p c t i", i=4),
                func=ACT.Abs,
            )

        woven = {}

        def subtract_woven(b, c0):
            inner = slice(c0 % BANK, c0 % BANK + P)
            woven[c0] = ring.tile([P, P, PACK], F32, name="woven", bufs=2)
            nc.vector.tensor_tensor(
                out=woven[c0][:], in0=names[b, c0, (0, 1, 2, 3)][0][:].rearrange("p t n -> p n t"),
                in1=reading[b, c0 // BANK][:, :, inner].rearrange("p t n -> p n t"), op=ALU.subtract,
            )

        def abs_on_vector(b, c0):
            h16[b, c0] = ring.tile([P, PACK * P], BF16, name="h16_last", align_bytes=64, bufs=2)
            flat = woven[c0][:].rearrange("p n t -> p (n t)")
            nc.vector.scalar_tensor_tensor(out=h16[b, c0][:], in0=flat, scalar=-1.0, in1=flat, op0=ALU.mult, op1=ALU.max)

        def quantize_h(b, c0, width):
            cols = slice(c0, c0 + width)
            nc.vector.quantize_mx(out=h_c[b][:, cols].bitcast(FP8X4), scales=h_s[b][:, cols], in_=h16[b, c0][:])

        def scores(c0, width, indices, store_each=False):
            per_bank = min(BINS, BANK // width)
            result = kept("result%d" % c0, [P, BINS, width], F32)
            for first, index in zip(range(0, BINS, per_bank), indices):
                bins = range(first, min(first + per_bank, BINS))
                acc = bank([P, len(bins), width], index)
                todo = [(b, c, n0) for b in range(GROUPS) for c in bins for n0 in range(0, width, P)]
                for b, c, n0 in todo:
                    cols = slice(c0 + n0, c0 + n0 + P)
                    nc.tensor.matmul_mx(
                        out=acc[:, c - first, n0 : n0 + P],
                        lhsT=w4_c[:, b, 2 * c * P : 2 * (c + 1) * P].bitcast(FP4X4), lhsT_scale=w4_s[:, b, c * P : (c + 1) * P],
                        rhs=h_c[b][:, cols].bitcast(FP8X4), rhs_scale=h_s[b][:, cols],
                        start=(b, c, n0) == todo[0], stop=(b, c, n0) == todo[-1],
                    )
                for c in bins:
                    nc.scalar.activation(out=result[:, c, :], in_=acc[:, c - first, :], func=ACT.Sigmoid, bias=bias_c[:, c : c + 1])
                    if store_each:
                        nc.sync.dma_start(out=out[c * P : (c + 1) * P, c0 : c0 + width], in_=result[:, c, :])
            if not store_each:
                nc.sync.dma_start(out=out[:, c0 : c0 + width].rearrange("(c p) n -> p c n", p=P), in_=result[:])

        def gather_words(a, on):
            picked_c[a] = placed("picked_c%d" % a, [P, S], U32, on)
            nc.vector.tensor_copy(picked_c[a][:], tab_c[a][:].indirect(offsets[:]))

        def gather_scales(on):
            picked_s[0] = placed("picked_s", [P, S], U8, on)
            nc.vector.tensor_copy(picked_s[0][:], tab_s[:].indirect(offsets[:]))

        W20, W21 = ("w2", 0, 0), ("w2", 0, 1)
        W00, W10, W01, W11 = ("w1", 0, 0), ("w1", 1, 0), ("w1", 0, 1), ("w1", 1, 1)
        tiles = [(half, t) for half in range(2) for t in range(PACK)]

        cast(W21, 0, "vector")
        cast(W21, 1, "scalar")
        quantize(W21, 0)
        quantize(W21, 1)
        reserve("first_pick", 4 * S)
        reserve("gates", 3 * GROUPED_BYTES)
        second_reading(1, *tiles[0])
        second_reading(1, *tiles[1])
        for i, tile in enumerate(tiles):
            larger_reading(1, *tile)
            if i + 2 < len(tiles):
                second_reading(1, *tiles[i + 2], "first_pick" if i + 2 == 7 else None)
            if i == 1:
                cast(W20, 1, "scalar", "read2_100")
            if i == 3:
                cast(W20, 0, "vector", "read2_102")
            if i == 4:
                quantize(W20, 1, "gates", CODE_BYTES, "gates", 2 * GROUPED_BYTES)
                quantize(W20, 0)
        second_reading(0, 0, 0)
        larger_reading(0, 0, 0)
        for tile in tiles[1:]:
            excess_reading(0, *tile)
        gather_words(0, "first_pick")
        gather_scales("tab_c0")
        gather_words(1, "tab_s")
        for q in range(4):
            for u in range(2):
                quarter_passes(0, q, u, (W20,))

        cast(W00, 0, "scalar", "codes_w2_0_0_1")
        cast(W00, 1, "scalar", "scales_w2_0_0_1")
        quantize(W00, 0, "tab_c1")
        cast(W10, 0, "vector", "grouped_w1_0_0_0", -CODE_BYTES)
        cast(W10, 1, "scalar", "grouped_w1_0_0_0", CODE_BYTES)
        quantize(W00, 1)
        quantize(W10, 0)
        quantize(W10, 1, "grouped_w1_1_0_0")
        for q in range(4):
            for u in range(2):
                quarter_passes(0, q, u, (W00, W10))
        cast(W01, 0, "scalar", "raw_w1_1_0", 2 * GROUPED_BYTES)
        cast(W01, 1, "scalar", "raw_w1_1_0")
        cast(W11, 1, "scalar", "raw_w1_0_1")
        for q in range(2):
            for u in range(2):
                subtract(0, q, u)
            abs_on_scalar(0, q)
        quantize(W01, 0, "reading000")
        subtract(0, 2, 0)
        cast(W11, 0, "vector", "grouped_w1_0_1_0", -CODE_BYTES)
        quantize(W01, 1, "grouped_w1_0_1_0", CODE_BYTES)
        subtract(0, 2, 1)
        abs_on_scalar(0, 2)
        quantize(W11, 0)
        quantize(W11, 1, "grouped_w1_0_1_1")

        for q in range(3):
            for u in range(2):
                quarter_passes(1, q, u, (W01, W11))
        subtract(0, 3, 0)
        subtract(1, 0, 0)
        quantize_h(0, 0, QUARTER)
        subtract(1, 0, 1)
        abs_on_scalar(1, 0)
        subtract(1, 1, 0)
        quantize_h(0, 256, QUARTER)
        subtract(1, 1, 1)
        abs_on_scalar(1, 1)
        subtract(0, 3, 1)
        quantize_h(0, 512, QUARTER)
        name_passes(1, 768, P, (0, 1, 2, 3), 6, (W01, W11))
        name_passes(1, 896, P, (0, 1, 2, 3), 7, (W01, W11))
        abs_on_scalar(0, 3)
        quantize_h(1, 0, QUARTER)
        scores(0, QUARTER, (0, 1))
        subtract(1, 2, 0)
        quantize_h(1, 256, QUARTER)
        subtract(1, 2, 1)
        abs_on_scalar(1, 2)
        scores(256, QUARTER, (2, 3), True)
        subtract_woven(1, 768)
        quantize_h(0, 768, QUARTER)
        subtract_woven(1, 896)
        abs_on_vector(1, 768)
        abs_on_vector(1, 896)
        quantize_h(1, 768, P)
        scores(768, P, (6,))
        quantize_h(1, 512, QUARTER)
        quantize_h(1, 896, P)
        scores(512, QUARTER, (4, 5), True)
        scores(896, P, (7,))
